import numpy as np
import ml_dtypes


def mxq(x, axis, fmt="e4m3"):
    dtype, down = {"e4m3": (ml_dtypes.float8_e4m3fn, 7), "e5m2": (ml_dtypes.float8_e5m2, 14)}[fmt]
    v = np.moveaxis(np.asarray(x, np.float32).astype(ml_dtypes.bfloat16).astype(np.float64), axis, -1)
    blocks = v.reshape(v.shape[:-1] + (-1, 32))
    amax = np.abs(blocks).max(-1, keepdims=True)
    byte = np.maximum(np.where(amax > 0, np.frexp(amax)[1] - 1 + 127, 0) - down, 1)
    scale = np.exp2(byte - 127.0)
    codes = (blocks / scale).astype(np.float32).astype(dtype).astype(np.float64)
    return np.moveaxis((codes * scale).reshape(v.shape), -1, axis)


WIDE = False


def mx_kscale(k):
    if not WIDE:
        return np.ones(k)
    levels = np.array([10, -10, 5, -5, 0])
    if k % 512:
        return np.exp2(np.random.permutation(np.resize(levels, k // 32))).repeat(32)
    a = np.empty((k // 512, 16))
    for p in range(k // 512):
        a[p, :8] = np.random.permutation(np.resize(levels, 8))
        for g in range(8):
            far = levels[np.abs(levels - a[p, g]) >= 10]
            a[p, g + 8] = far[np.random.randint(len(far))]
    return np.exp2(a.ravel()).repeat(32)


def f64(x):
    return np.asarray(x).astype(np.float64)


def striped(idx):
    return np.tile(idx.reshape(-1, 16).T, (8, 1)).astype(np.uint16)


def unstriped(offs):
    return offs[:16].T.reshape(-1).astype(np.int64)


E2M1 = np.array([0.0, 0.5, 1.0, 1.5, 2.0, 3.0, 4.0, 6.0, -0.0, -0.5, -1.0, -1.5, -2.0, -3.0, -4.0, -6.0])


def pack_weight(w, fmt):
    k, n = w.shape
    w = f64(np.asarray(w, np.float32).astype(ml_dtypes.bfloat16)).reshape(k // 32, 32, n)
    amax = np.abs(w).max(1)
    if fmt == "e4m3":
        byte = np.frexp(amax)[1] - 1 + 127 - 7
    else:
        mant, ex = np.frexp(amax / 6.0)
        byte = np.where(mant > 0.5, ex, ex - 1) + 127
    byte = np.clip(np.where(amax > 0, byte, 1), 1, 254)
    scaled = (w * np.exp2(127.0 - byte)[:, None, :]).reshape(k, n).astype(np.float32)
    by_word = np.ascontiguousarray(scaled.reshape(k // 512, 128, 4, n).transpose(0, 1, 3, 2))
    if fmt == "e4m3":
        words = by_word.astype(ml_dtypes.float8_e4m3fn).view(np.uint8)
    else:
        c = by_word.astype(ml_dtypes.float4_e2m1fn).view(np.uint8) & 0xF
        words = (c[..., 0::2] | (c[..., 1::2] << 4)).reshape(k // 512, 128, 2 * n)
    return np.ascontiguousarray(words), np.ascontiguousarray(byte.astype(np.uint8).reshape(k // 512, 16, n))


def unpack_weight(words, scales, fmt):
    g, _, n = scales.shape
    words = np.ascontiguousarray(words).reshape(g, 128, n, -1)
    if fmt == "e4m3":
        vals = words.view(ml_dtypes.float8_e4m3fn).astype(np.float64)
    else:
        nib = np.empty((g, 128, n, 4), np.uint8)
        nib[..., 0::2] = words & 0xF
        nib[..., 1::2] = words >> 4
        vals = E2M1[nib]
    vals = vals * np.repeat(np.exp2(scales.astype(np.float64) - 127.0), 8, axis=1)[..., None]
    return vals.transpose(0, 1, 3, 2).reshape(g * 512, n)


def gelu(v):
    return 0.5 * v * (1.0 + np.tanh(np.sqrt(2.0 / np.pi) * (v + 0.044715 * v**3)))


K, M, T, S = 1024, 512, 4096, 2048


def setup_inputs():
    n = np.random.standard_normal
    s = mx_kscale(K)[:, None]
    v = pack_weight(n((K, T)) * s, "e4m3")
    return {
        "tab_words": v[0],
        "tab_scales": v[1],
        "w": (n((K, M)) / np.sqrt(K) / s).astype(np.float32),
        "ts": np.tile(np.exp(0.5 * n(T)), (128, 1)).astype(np.float32),
        "b": (0.3 * n(512)).astype(np.float32),
        "offs": striped(np.random.permutation(T)[:S]),
    }


def reference(tab_words, tab_scales, w, ts, b, offs):
    tab_ = unpack_weight(tab_words, tab_scales, "e4m3")[:, unstriped(offs)]
    w_ = mxq(f64(w), 0, "e4m3")
    y = w_.T @ tab_
    y = y * f64(ts)[0][unstriped(offs)]
    return gelu(y + f64(b)[:, None])

@@ -1,0 +1,185 @@
+from contextlib import ExitStack
+
+import concourse.mybir as mybir
+from concourse.masks import make_identity
+
+K, M, T, S = 1024, 512, 4096, 2048
+FLOPS = 2 * K * M * S
+BYTES = K * T + (K // 32) * T + 4 * K * M + 4 * T + 4 * M + 2 * 128 * (S // 16) + 4 * M * S
+
+F32 = mybir.dt.float32
+BF16 = mybir.dt.bfloat16
+I32 = mybir.dt.int32
+U32 = mybir.dt.uint32
+U16 = mybir.dt.uint16
+U8 = mybir.dt.uint8
+FP8X4 = mybir.dt.float8_e4m3fn_x4
+ACT = mybir.ActivationFunctionType
+MULT = mybir.AluOpType.mult
+
+P = 128
+PASSES = K // 512
+N_TILES = M // P
+BANK = 512
+TURNED = (256, 256)
+DIRECT = (512, 512, 512)
+TS_ROW = P - 1
+LAST = S // BANK - 1
+
+
+def spans(widths, first):
+    result = []
+    for width in widths:
+        result.append((first, width))
+        first = first + width
+    return result
+
+
+def tile_list_tabts_gelu_kernel(tc, tab_words, tab_scales, w, ts, b, offs, out):
+    nc = tc.nc
+    turned = spans(TURNED, 0)
+    direct = spans(DIRECT, sum(TURNED))
+    direct0 = sum(TURNED)
+
+    with ExitStack() as ctx:
+        keep = ctx.enter_context(tc.tile_pool(name="keep", bufs=1))
+        ring = ctx.enter_context(tc.tile_pool(name="ring", bufs=4))
+        psum = ctx.enter_context(tc.psum_pool(name="psum", bufs=4))
+
+        offsets = keep.tile([P, S // 16], U16, name="offsets")
+        ts_win = keep.tile([P, T], F32, name="ts_win")
+        scale_win = keep.tile([P, T], U8, name="scale_win")
+        word_win = [keep.tile([P, T], U32, name="word_win%d" % a) for a in range(PASSES)]
+        w_raw = [keep.tile([P, 4, M], F32, name="w_raw%d" % a) for a in range(PASSES)]
+        bias = keep.tile([P, N_TILES], F32, name="bias")
+        ident = keep.tile([P, P], F32, name="ident")
+
+        def picked(window, j0, width):
+            return window[:].indirect(offsets[:, j0 // 16 : (j0 + width) // 16])
+
+        nc.vector.memset(scale_win[:].bitcast(I32), 0)
+        nc.vector.memset(ts_win[0:TS_ROW, :], 0.0)
+        make_identity(nc, ident[:])
+
+        nc.sync.dma_start(offsets[:], offs)
+        nc.sync.dma_start(out=ts_win[TS_ROW:P, :], in_=ts[0:1, :])
+        for q in range(4):
+            nc.gpsimd.dma_start(
+                out=scale_win[32 * q : 32 * q + 4 * PASSES, :].bitcast(I32),
+                in_=tab_scales[:, 4 * q : 4 * q + 4, :].bitcast(I32),
+            )
+
+        def load_words(a):
+            nc.sync.dma_start(
+                out=word_win[a][:].bitcast(I32),
+                in_=tab_words[a].rearrange("p t i -> p (t i)").bitcast(I32),
+            )
+
+        load_words(0)
+        for a in range(PASSES):
+            nc.sync.dma_start(out=w_raw[a][:], in_=w[512 * a : 512 * (a + 1), :].rearrange("(p i) n -> p i n", i=4))
+        load_words(1)
+        with nc.allow_non_contiguous_dma(reason="one bias value a partition"):
+            nc.sync.dma_start(out=bias[:], in_=b.rearrange("(t p) -> p t", p=P))
+
+        ts_picked = keep.tile([P, S], F32, name="ts_picked")
+        nc.vector.tensor_copy(out=ts_picked[:], in_=picked(ts_win, 0, S))
+        words = {}
+        scales = {}
+
+        def gather_words(a, g, tag, pieces=1):
+            words[a, g] = keep.tile([P, BANK], U32, name="words%d_%d" % (a, g), tag=tag, align_bytes=64)
+            width = BANK // pieces
+            for j in range(0, BANK, width):
+                nc.vector.tensor_copy(out=words[a, g][:, j : j + width], in_=picked(word_win[a], g * BANK + j, width))
+
+        def gather_scales(g, tag):
+            scales[g] = keep.tile([P, BANK], U8, name="scales%d" % g, tag=tag, align_bytes=64)
+            nc.vector.tensor_copy(out=scales[g][:], in_=picked(scale_win, g * BANK, BANK))
+
+        for g in range(LAST):
+            gather_words(0, g, "words0_%d" % g)
+        for g in range(LAST):
+            gather_scales(g, "scales%d" % g)
+
+        ts_col = keep.tile([P, S // P], F32, name="ts_col")
+        for g in range(S // BANK):
+            bank = psum.tile([P, 4, P], F32, name="bank_t", tag="turn")
+            for i in range(4):
+                c = 4 * g + i
+                nc.tensor.transpose(bank[:, i, :], ts_picked[:, c * P : (c + 1) * P], ident[:])
+            nc.scalar.copy(out=ts_col[:, 4 * g : 4 * g + 4], in_=bank[:, :, TS_ROW])
+        ts_rows = keep.tile([P, S - direct0], F32, name="ts_rows")
+        for j0, width in direct:
+            bank = psum.tile([P, BANK], F32, name="bank_r", tag="turn")
+            for i in range(width // P):
+                c = j0 // P + i
+                nc.tensor.transpose(bank[:, i * P : (i + 1) * P], ts_col[:, c : c + 1].to_broadcast([P, P]), ident[:])
+            nc.scalar.copy(out=ts_rows[:, j0 - direct0 : j0 - direct0 + width], in_=bank[:, 0:width])
+
+        w_codes = []
+        w_scales = []
+        for a in range(PASSES):
+            grouped = keep.tile([P, M, 4], BF16, name="grouped%d" % a, align_bytes=64)
+            nc.scalar.copy(
+                out=grouped[:].rearrange("p (c e) i -> p c i e", e=4),
+                in_=w_raw[a][:].rearrange("p i (c e) -> p c i e", e=4),
+            )
+            codes = keep.tile([P, M], U32, name="w_codes%d" % a, align_bytes=64)
+            plane = keep.tile([P, M], U8, name="w_scales%d" % a, align_bytes=64)
+            nc.vector.quantize_mx(out=codes[:].bitcast(FP8X4), scales=plane[:], in_=grouped[:].rearrange("p n i -> p (n i)"))
+            w_codes.append(codes)
+            w_scales.append(plane)
+
+        gather_words(1, 0, "words1_0", pieces=2)
+        for g in range(1, LAST + 1):
+            gather_words(1, g, "words1_%d" % g)
+
+        def table_operand(a, j0, width):
+            g, j = divmod(j0, BANK)
+            return words[a, g][:, j : j + width].bitcast(FP8X4), scales[g][4 * a : P, j : j + width]
+
+        def weight_operand(a, n0, width):
+            return w_codes[a][:, n0 : n0 + width].bitcast(FP8X4), w_scales[a][:, n0 : n0 + width]
+
+        def product(acc, stationary, moving):
+            for a in range(PASSES):
+                lhs, lhs_scale = stationary(a)
+                rhs, rhs_scale = moving(a)
+                nc.tensor.matmul_mx(
+                    out=acc, lhsT=lhs, lhsT_scale=lhs_scale, rhs=rhs, rhs_scale=rhs_scale,
+                    start=(a == 0), stop=(a == PASSES - 1),
+                )
+
+        scaled = {}
+        for j0, width in turned:
+            for c in range(j0 // P, (j0 + width) // P):
+                acc = psum.tile([P, M], F32, name="acc_t", tag="sum")
+                product(acc[:], lambda a: table_operand(a, c * P, P), lambda a: weight_operand(a, 0, M))
+                scaled[c] = ring.tile([P, M], F32, name="scaled")
+                nc.scalar.activation(out=scaled[c][:], in_=acc[:], func=ACT.Copy, scale=ts_col[:, c : c + 1])
+        gather_words(0, LAST, "words1_0")
+        gather_scales(LAST, "scales0")
+        for j0, width in turned:
+            result = ring.tile([P, N_TILES, width], F32, name="result_t")
+            for pair in range(N_TILES // 2):
+                bank = psum.tile([P, 2, width], F32, name="bank_y", tag="turn")
+                for h in range(2):
+                    n0 = (2 * pair + h) * P
+                    for i in range(width // P):
+                        nc.tensor.transpose(bank[:, h, i * P : (i + 1) * P], scaled[j0 // P + i][:, n0 : n0 + P], ident[:])
+                for h in range(2):
+                    t = 2 * pair + h
+                    nc.scalar.activation(out=result[:, t, :], in_=bank[:, h, :], func=ACT.Gelu_apprx_tanh, bias=bias[:, t : t + 1])
+            nc.sync.dma_start(out=out[:, j0 : j0 + width].rearrange("(t p) j -> p t j", p=P), in_=result[:])
+
+        for r, (j0, width) in enumerate(direct):
+            for t in range(N_TILES):
+                acc = psum.tile([P, width], F32, name="acc_d", tag=("sum", "turn")[r % 2])
+                for j, part in spans([x for x in (512, 256, 128) if width & x], 0):
+                    product(acc[:, j : j + part], lambda a: weight_operand(a, t * P, P), lambda a: table_operand(a, j0 + j, part))
+                y = ring.tile([P, width], F32, name="y")
+                nc.vector.tensor_tensor(out=y[:], in0=acc[:], in1=ts_rows[:, j0 - direct0 : j0 - direct0 + width], op=MULT)
+                result = keep.tile([P, width], F32, name="result_d%d_%d" % (r, t))
+                nc.scalar.activation(out=result[:], in_=y[:], func=ACT.Gelu_apprx_tanh, bias=bias[:, t : t + 1])
+                nc.sync.dma_start(out=out[t * P : (t + 1) * P, j0 : j0 + width], in_=result[:])

@@ -24,7 +24,6 @@ BANK = 512
 TURNED = (256, 256)
 DIRECT = (512, 512, 512)
 TS_ROW = P - 1
-LAST = S // BANK - 1
 
 
 def spans(widths, first):
@@ -63,11 +62,6 @@ def tile_list_tabts_gelu_kernel(tc, tab_words, tab_scales, w, ts, b, offs, out):
 
         nc.sync.dma_start(offsets[:], offs)
         nc.sync.dma_start(out=ts_win[TS_ROW:P, :], in_=ts[0:1, :])
-        for q in range(4):
-            nc.gpsimd.dma_start(
-                out=scale_win[32 * q : 32 * q + 4 * PASSES, :].bitcast(I32),
-                in_=tab_scales[:, 4 * q : 4 * q + 4, :].bitcast(I32),
-            )
 
         def load_words(a):
             nc.sync.dma_start(
@@ -76,6 +70,11 @@ def tile_list_tabts_gelu_kernel(tc, tab_words, tab_scales, w, ts, b, offs, out):
             )
 
         load_words(0)
+        for q in range(4):
+            nc.sync.dma_start(
+                out=scale_win[32 * q : 32 * q + 4 * PASSES, :].bitcast(I32),
+                in_=tab_scales[:, 4 * q : 4 * q + 4, :].bitcast(I32),
+            )
         for a in range(PASSES):
             nc.sync.dma_start(out=w_raw[a][:], in_=w[512 * a : 512 * (a + 1), :].rearrange("(p i) n -> p i n", i=4))
         load_words(1)
@@ -84,23 +83,10 @@ def tile_list_tabts_gelu_kernel(tc, tab_words, tab_scales, w, ts, b, offs, out):
 
         ts_picked = keep.tile([P, S], F32, name="ts_picked")
         nc.vector.tensor_copy(out=ts_picked[:], in_=picked(ts_win, 0, S))
-        words = {}
-        scales = {}
-
-        def gather_words(a, g, tag, pieces=1):
-            words[a, g] = keep.tile([P, BANK], U32, name="words%d_%d" % (a, g), tag=tag, align_bytes=64)
-            width = BANK // pieces
-            for j in range(0, BANK, width):
-                nc.vector.tensor_copy(out=words[a, g][:, j : j + width], in_=picked(word_win[a], g * BANK + j, width))
-
-        def gather_scales(g, tag):
-            scales[g] = keep.tile([P, BANK], U8, name="scales%d" % g, tag=tag, align_bytes=64)
-            nc.vector.tensor_copy(out=scales[g][:], in_=picked(scale_win, g * BANK, BANK))
-
-        for g in range(LAST):
-            gather_words(0, g, "words0_%d" % g)
-        for g in range(LAST):
-            gather_scales(g, "scales%d" % g)
+        words = [keep.tile([P, S], U32, name="words%d" % a, align_bytes=64) for a in range(PASSES)]
+        scales = keep.tile([P, S], U8, name="scales", align_bytes=64)
+        nc.vector.tensor_copy(out=words[0][:], in_=picked(word_win[0], 0, S))
+        nc.vector.tensor_copy(out=scales[:], in_=picked(scale_win, 0, S))
 
         ts_col = keep.tile([P, S // P], F32, name="ts_col")
         for g in range(S // BANK):
@@ -121,23 +107,18 @@ def tile_list_tabts_gelu_kernel(tc, tab_words, tab_scales, w, ts, b, offs, out):
         w_scales = []
         for a in range(PASSES):
             grouped = keep.tile([P, M, 4], BF16, name="grouped%d" % a, align_bytes=64)
-            nc.scalar.copy(
-                out=grouped[:].rearrange("p (c e) i -> p c i e", e=4),
-                in_=w_raw[a][:].rearrange("p i (c e) -> p c i e", e=4),
-            )
+            nc.scalar.copy(out=grouped[:], in_=w_raw[a][:].rearrange("p i n -> p n i"))
             codes = keep.tile([P, M], U32, name="w_codes%d" % a, align_bytes=64)
             plane = keep.tile([P, M], U8, name="w_scales%d" % a, align_bytes=64)
             nc.vector.quantize_mx(out=codes[:].bitcast(FP8X4), scales=plane[:], in_=grouped[:].rearrange("p n i -> p (n i)"))
             w_codes.append(codes)
             w_scales.append(plane)
 
-        gather_words(1, 0, "words1_0", pieces=2)
-        for g in range(1, LAST + 1):
-            gather_words(1, g, "words1_%d" % g)
+        for j0, width in turned + direct:
+            nc.vector.tensor_copy(out=words[1][:, j0 : j0 + width], in_=picked(word_win[1], j0, width))
 
         def table_operand(a, j0, width):
-            g, j = divmod(j0, BANK)
-            return words[a, g][:, j : j + width].bitcast(FP8X4), scales[g][4 * a : P, j : j + width]
+            return words[a][:, j0 : j0 + width].bitcast(FP8X4), scales[4 * a : P, j0 : j0 + width]
 
         def weight_operand(a, n0, width):
             return w_codes[a][:, n0 : n0 + width].bitcast(FP8X4), w_scales[a][:, n0 : n0 + width]
@@ -151,6 +132,10 @@ def tile_list_tabts_gelu_kernel(tc, tab_words, tab_scales, w, ts, b, offs, out):
                     start=(a == 0), stop=(a == PASSES - 1),
                 )
 
+        def store(result, t0, tiles, j0, width):
+            rows = out[t0 * P : (t0 + tiles) * P, j0 : j0 + width]
+            nc.sync.dma_start(out=rows.rearrange("(t p) j -> p t j", p=P), in_=result[:])
+
         scaled = {}
         for j0, width in turned:
             for c in range(j0 // P, (j0 + width) // P):
@@ -158,11 +143,9 @@ def tile_list_tabts_gelu_kernel(tc, tab_words, tab_scales, w, ts, b, offs, out):
                 product(acc[:], lambda a: table_operand(a, c * P, P), lambda a: weight_operand(a, 0, M))
                 scaled[c] = ring.tile([P, M], F32, name="scaled")
                 nc.scalar.activation(out=scaled[c][:], in_=acc[:], func=ACT.Copy, scale=ts_col[:, c : c + 1])
-        gather_words(0, LAST, "words1_0")
-        gather_scales(LAST, "scales0")
         for j0, width in turned:
-            result = ring.tile([P, N_TILES, width], F32, name="result_t")
             for pair in range(N_TILES // 2):
+                result = ring.tile([P, 2, width], F32, name="result_t")
                 bank = psum.tile([P, 2, width], F32, name="bank_y", tag="turn")
                 for h in range(2):
                     n0 = (2 * pair + h) * P
@@ -170,16 +153,18 @@ def tile_list_tabts_gelu_kernel(tc, tab_words, tab_scales, w, ts, b, offs, out):
                         nc.tensor.transpose(bank[:, h, i * P : (i + 1) * P], scaled[j0 // P + i][:, n0 : n0 + P], ident[:])
                 for h in range(2):
                     t = 2 * pair + h
-                    nc.scalar.activation(out=result[:, t, :], in_=bank[:, h, :], func=ACT.Gelu_apprx_tanh, bias=bias[:, t : t + 1])
-            nc.sync.dma_start(out=out[:, j0 : j0 + width].rearrange("(t p) j -> p t j", p=P), in_=result[:])
+                    nc.scalar.activation(out=result[:, h, :], in_=bank[:, h, :], func=ACT.Gelu_apprx_tanh, bias=bias[:, t : t + 1])
+                store(result, 2 * pair, 2, j0, width)
 
         for r, (j0, width) in enumerate(direct):
             for t in range(N_TILES):
                 acc = psum.tile([P, width], F32, name="acc_d", tag=("sum", "turn")[r % 2])
-                for j, part in spans([x for x in (512, 256, 128) if width & x], 0):
-                    product(acc[:, j : j + part], lambda a: weight_operand(a, t * P, P), lambda a: table_operand(a, j0 + j, part))
-                y = ring.tile([P, width], F32, name="y")
+                product(acc[:], lambda a: weight_operand(a, t * P, P), lambda a: table_operand(a, j0, width))
+                y = keep.tile([P, width], F32, name="y%d_%d" % (r, t))
                 nc.vector.tensor_tensor(out=y[:], in0=acc[:], in1=ts_rows[:, j0 - direct0 : j0 - direct0 + width], op=MULT)
-                result = keep.tile([P, width], F32, name="result_d%d_%d" % (r, t))
-                nc.scalar.activation(out=result[:], in_=y[:], func=ACT.Gelu_apprx_tanh, bias=bias[:, t : t + 1])
-                nc.sync.dma_start(out=out[t * P : (t + 1) * P, j0 : j0 + width], in_=result[:])
+                tiles = 1 if r == len(direct) - 1 else 2
+                if t % tiles == 0:
+                    result = keep.tile([P, tiles, width], F32, name="result_d%d_%d" % (r, t))
+                nc.scalar.activation(out=result[:, t % tiles, :], in_=y[:], func=ACT.Gelu_apprx_tanh, bias=bias[:, t : t + 1])
+                if t % tiles == tiles - 1:
+                    store(result, t - tiles + 1, tiles, j0, width)

@@ -24,6 +24,7 @@ BANK = 512
 TURNED = (256, 256)
 DIRECT = (512, 512, 512)
 TS_ROW = P - 1
+TS_SPLIT = 1832
 
 
 def spans(widths, first):
@@ -56,9 +57,15 @@ def tile_list_tabts_gelu_kernel(tc, tab_words, tab_scales, w, ts, b, offs, out):
         def picked(window, j0, width):
             return window[:].indirect(offsets[:, j0 // 16 : (j0 + width) // 16])
 
-        nc.vector.memset(scale_win[:].bitcast(I32), 0)
-        nc.vector.memset(ts_win[0:TS_ROW, :], 0.0)
+        nc.gpsimd.memset(scale_win[:].bitcast(I32), 0)
+        nc.gpsimd.memset(ts_win[0:TS_ROW, 0:TS_SPLIT], 0.0)
+        nc.vector.memset(ts_win[0:TS_ROW, TS_SPLIT : T - 1], 0.0)
+        nc.vector.memset(ts_win[0:TS_ROW, T - 1 : T], 0.0)
         make_identity(nc, ident[:])
+
+        warm = keep.tile([P, 2], F32, name="warm")
+        nc.vector.memset(warm[:, 0:1], 0.0)
+        nc.scalar.activation(out=warm[:, 1:2], in_=warm[:, 0:1], func=ACT.Gelu_apprx_tanh)
 
         nc.sync.dma_start(offsets[:], offs)
         nc.sync.dma_start(out=ts_win[TS_ROW:P, :], in_=ts[0:1, :])
@@ -69,26 +76,43 @@ def tile_list_tabts_gelu_kernel(tc, tab_words, tab_scales, w, ts, b, offs, out):
                 in_=tab_words[a].rearrange("p t i -> p (t i)").bitcast(I32),
             )
 
-        load_words(0)
+        def load_weights(a):
+            nc.sync.dma_start(out=w_raw[a][:], in_=w[512 * a : 512 * (a + 1), :].rearrange("(p i) n -> p i n", i=4))
+
+        load_weights(0)
         for q in range(4):
             nc.sync.dma_start(
                 out=scale_win[32 * q : 32 * q + 4 * PASSES, :].bitcast(I32),
                 in_=tab_scales[:, 4 * q : 4 * q + 4, :].bitcast(I32),
             )
-        for a in range(PASSES):
-            nc.sync.dma_start(out=w_raw[a][:], in_=w[512 * a : 512 * (a + 1), :].rearrange("(p i) n -> p i n", i=4))
+        load_words(0)
+        load_weights(1)
         load_words(1)
         with nc.allow_non_contiguous_dma(reason="one bias value a partition"):
             nc.sync.dma_start(out=bias[:], in_=b.rearrange("(t p) -> p t", p=P))
 
+        w_codes = []
+        w_scales = []
+
+        def quantise_weights(a):
+            grouped = keep.tile([P, M, 4], BF16, name="grouped%d" % a, align_bytes=64)
+            nc.scalar.copy(out=grouped[:], in_=w_raw[a][:].rearrange("p i n -> p n i"))
+            codes = keep.tile([P, M], U32, name="w_codes%d" % a, align_bytes=64)
+            plane = keep.tile([P, M], U8, name="w_scales%d" % a, align_bytes=64)
+            nc.vector.quantize_mx(out=codes[:].bitcast(FP8X4), scales=plane[:], in_=grouped[:].rearrange("p n i -> p (n i)"))
+            w_codes.append(codes)
+            w_scales.append(plane)
+
+        quantise_weights(0)
         ts_picked = keep.tile([P, S], F32, name="ts_picked")
         nc.vector.tensor_copy(out=ts_picked[:], in_=picked(ts_win, 0, S))
         words = [keep.tile([P, S], U32, name="words%d" % a, align_bytes=64) for a in range(PASSES)]
         scales = keep.tile([P, S], U8, name="scales", align_bytes=64)
-        nc.vector.tensor_copy(out=words[0][:], in_=picked(word_win[0], 0, S))
         nc.vector.tensor_copy(out=scales[:], in_=picked(scale_win, 0, S))
+        for j0 in range(0, S, BANK):
+            nc.vector.tensor_copy(out=words[0][:, j0 : j0 + BANK], in_=picked(word_win[0], j0, BANK))
 
-        ts_col = keep.tile([P, S // P], F32, name="ts_col")
+        ts_col = keep.tile([P, S // P], F32, name="ts_col", tag="w_raw0")
         for g in range(S // BANK):
             bank = psum.tile([P, 4, P], F32, name="bank_t", tag="turn")
             for i in range(4):
@@ -103,16 +127,8 @@ def tile_list_tabts_gelu_kernel(tc, tab_words, tab_scales, w, ts, b, offs, out):
                 nc.tensor.transpose(bank[:, i * P : (i + 1) * P], ts_col[:, c : c + 1].to_broadcast([P, P]), ident[:])
             nc.scalar.copy(out=ts_rows[:, j0 - direct0 : j0 - direct0 + width], in_=bank[:, 0:width])
 
-        w_codes = []
-        w_scales = []
-        for a in range(PASSES):
-            grouped = keep.tile([P, M, 4], BF16, name="grouped%d" % a, align_bytes=64)
-            nc.scalar.copy(out=grouped[:], in_=w_raw[a][:].rearrange("p i n -> p n i"))
-            codes = keep.tile([P, M], U32, name="w_codes%d" % a, align_bytes=64)
-            plane = keep.tile([P, M], U8, name="w_scales%d" % a, align_bytes=64)
-            nc.vector.quantize_mx(out=codes[:].bitcast(FP8X4), scales=plane[:], in_=grouped[:].rearrange("p n i -> p (n i)"))
-            w_codes.append(codes)
-            w_scales.append(plane)
+        for a in range(1, PASSES):
+            quantise_weights(a)
 
         for j0, width in turned + direct:
             nc.vector.tensor_copy(out=words[1][:, j0 : j0 + width], in_=picked(word_win[1], j0, width))
@@ -146,7 +162,7 @@ def tile_list_tabts_gelu_kernel(tc, tab_words, tab_scales, w, ts, b, offs, out):
         for j0, width in turned:
             for pair in range(N_TILES // 2):
                 result = ring.tile([P, 2, width], F32, name="result_t")
-                bank = psum.tile([P, 2, width], F32, name="bank_y", tag="turn")
+                bank = psum.tile([P, 2, width], F32, name="bank_y", tag="sum")
                 for h in range(2):
                     n0 = (2 * pair + h) * P
                     for i in range(width // P):
@@ -158,9 +174,9 @@ def tile_list_tabts_gelu_kernel(tc, tab_words, tab_scales, w, ts, b, offs, out):
 
         for r, (j0, width) in enumerate(direct):
             for t in range(N_TILES):
-                acc = psum.tile([P, width], F32, name="acc_d", tag=("sum", "turn")[r % 2])
+                acc = psum.tile([P, width], F32, name="acc_d", tag=("turn", "sum")[r % 2])
                 product(acc[:], lambda a: weight_operand(a, t * P, P), lambda a: table_operand(a, j0, width))
-                y = keep.tile([P, width], F32, name="y%d_%d" % (r, t))
+                y = ring.tile([P, width], F32, name="y", tag="scaled")
                 nc.vector.tensor_tensor(out=y[:], in0=acc[:], in1=ts_rows[:, j0 - direct0 : j0 - direct0 + width], op=MULT)
                 tiles = 1 if r == len(direct) - 1 else 2
                 if t % tiles == 0:

from contextlib import ExitStack

import concourse.mybir as mybir
from concourse.masks import make_identity

K, M, T, S = 1024, 512, 4096, 2048
FLOPS = 2 * K * M * S
BYTES = K * T + (K // 32) * T + 4 * K * M + 4 * T + 4 * M + 2 * 128 * (S // 16) + 4 * M * S

F32 = mybir.dt.float32
BF16 = mybir.dt.bfloat16
I32 = mybir.dt.int32
U32 = mybir.dt.uint32
U16 = mybir.dt.uint16
U8 = mybir.dt.uint8
FP8X4 = mybir.dt.float8_e4m3fn_x4
ACT = mybir.ActivationFunctionType
MULT = mybir.AluOpType.mult

P = 128
PASSES = K // 512
N_TILES = M // P
BANK = 512
TURNED = (256, 256)
DIRECT = (512, 512, 512)
TS_ROW = P - 1
TS_SPLIT = 1832


def spans(widths, first):
    result = []
    for width in widths:
        result.append((first, width))
        first = first + width
    return result


def tile_list_tabts_gelu_kernel(tc, tab_words, tab_scales, w, ts, b, offs, out):
    nc = tc.nc
    turned = spans(TURNED, 0)
    direct = spans(DIRECT, sum(TURNED))
    direct0 = sum(TURNED)

    with ExitStack() as ctx:
        keep = ctx.enter_context(tc.tile_pool(name="keep", bufs=1))
        ring = ctx.enter_context(tc.tile_pool(name="ring", bufs=4))
        psum = ctx.enter_context(tc.psum_pool(name="psum", bufs=4))

        offsets = keep.tile([P, S // 16], U16, name="offsets")
        ts_win = keep.tile([P, T], F32, name="ts_win")
        scale_win = keep.tile([P, T], U8, name="scale_win")
        word_win = [keep.tile([P, T], U32, name="word_win%d" % a) for a in range(PASSES)]
        w_raw = [keep.tile([P, 4, M], F32, name="w_raw%d" % a) for a in range(PASSES)]
        bias = keep.tile([P, N_TILES], F32, name="bias")
        ident = keep.tile([P, P], F32, name="ident")

        def picked(window, j0, width):
            return window[:].indirect(offsets[:, j0 // 16 : (j0 + width) // 16])

        nc.gpsimd.memset(scale_win[:].bitcast(I32), 0)
        nc.gpsimd.memset(ts_win[0:TS_ROW, 0:TS_SPLIT], 0.0)
        nc.vector.memset(ts_win[0:TS_ROW, TS_SPLIT : T - 1], 0.0)
        nc.vector.memset(ts_win[0:TS_ROW, T - 1 : T], 0.0)
        make_identity(nc, ident[:])

        warm = keep.tile([P, 2], F32, name="warm")
        nc.vector.memset(warm[:, 0:1], 0.0)
        nc.scalar.activation(out=warm[:, 1:2], in_=warm[:, 0:1], func=ACT.Gelu_apprx_tanh)

        nc.sync.dma_start(offsets[:], offs)
        nc.sync.dma_start(out=ts_win[TS_ROW:P, :], in_=ts[0:1, :])

        def load_words(a):
            nc.sync.dma_start(
                out=word_win[a][:].bitcast(I32),
                in_=tab_words[a].rearrange("p t i -> p (t i)").bitcast(I32),
            )

        def load_weights(a):
            nc.sync.dma_start(out=w_raw[a][:], in_=w[512 * a : 512 * (a + 1), :].rearrange("(p i) n -> p i n", i=4))

        load_weights(0)
        for q in range(4):
            nc.sync.dma_start(
                out=scale_win[32 * q : 32 * q + 4 * PASSES, :].bitcast(I32),
                in_=tab_scales[:, 4 * q : 4 * q + 4, :].bitcast(I32),
            )
        load_words(0)
        load_weights(1)
        load_words(1)
        with nc.allow_non_contiguous_dma(reason="one bias value a partition"):
            nc.sync.dma_start(out=bias[:], in_=b.rearrange("(t p) -> p t", p=P))

        w_codes = []
        w_scales = []

        def quantise_weights(a):
            grouped = keep.tile([P, M, 4], BF16, name="grouped%d" % a, align_bytes=64)
            nc.scalar.copy(out=grouped[:], in_=w_raw[a][:].rearrange("p i n -> p n i"))
            codes = keep.tile([P, M], U32, name="w_codes%d" % a, align_bytes=64)
            plane = keep.tile([P, M], U8, name="w_scales%d" % a, align_bytes=64)
            nc.vector.quantize_mx(out=codes[:].bitcast(FP8X4), scales=plane[:], in_=grouped[:].rearrange("p n i -> p (n i)"))
            w_codes.append(codes)
            w_scales.append(plane)

        quantise_weights(0)
        ts_picked = keep.tile([P, S], F32, name="ts_picked")
        nc.vector.tensor_copy(out=ts_picked[:], in_=picked(ts_win, 0, S))
        words = [keep.tile([P, S], U32, name="words%d" % a, align_bytes=64) for a in range(PASSES)]
        scales = keep.tile([P, S], U8, name="scales", align_bytes=64)
        nc.vector.tensor_copy(out=scales[:], in_=picked(scale_win, 0, S))
        for j0 in range(0, S, BANK):
            nc.vector.tensor_copy(out=words[0][:, j0 : j0 + BANK], in_=picked(word_win[0], j0, BANK))

        ts_col = keep.tile([P, S // P], F32, name="ts_col", tag="w_raw0")
        for g in range(S // BANK):
            bank = psum.tile([P, 4, P], F32, name="bank_t", tag="turn")
            for i in range(4):
                c = 4 * g + i
                nc.tensor.transpose(bank[:, i, :], ts_picked[:, c * P : (c + 1) * P], ident[:])
            nc.scalar.copy(out=ts_col[:, 4 * g : 4 * g + 4], in_=bank[:, :, TS_ROW])
        ts_rows = keep.tile([P, S - direct0], F32, name="ts_rows")
        for j0, width in direct:
            bank = psum.tile([P, BANK], F32, name="bank_r", tag="turn")
            for i in range(width // P):
                c = j0 // P + i
                nc.tensor.transpose(bank[:, i * P : (i + 1) * P], ts_col[:, c : c + 1].to_broadcast([P, P]), ident[:])
            nc.scalar.copy(out=ts_rows[:, j0 - direct0 : j0 - direct0 + width], in_=bank[:, 0:width])

        for a in range(1, PASSES):
            quantise_weights(a)

        for j0, width in turned + direct:
            nc.vector.tensor_copy(out=words[1][:, j0 : j0 + width], in_=picked(word_win[1], j0, width))

        def table_operand(a, j0, width):
            return words[a][:, j0 : j0 + width].bitcast(FP8X4), scales[4 * a : P, j0 : j0 + width]

        def weight_operand(a, n0, width):
            return w_codes[a][:, n0 : n0 + width].bitcast(FP8X4), w_scales[a][:, n0 : n0 + width]

        def product(acc, stationary, moving):
            for a in range(PASSES):
                lhs, lhs_scale = stationary(a)
                rhs, rhs_scale = moving(a)
                nc.tensor.matmul_mx(
                    out=acc, lhsT=lhs, lhsT_scale=lhs_scale, rhs=rhs, rhs_scale=rhs_scale,
                    start=(a == 0), stop=(a == PASSES - 1),
                )

        def store(result, t0, tiles, j0, width):
            rows = out[t0 * P : (t0 + tiles) * P, j0 : j0 + width]
            nc.sync.dma_start(out=rows.rearrange("(t p) j -> p t j", p=P), in_=result[:])

        scaled = {}
        for j0, width in turned:
            for c in range(j0 // P, (j0 + width) // P):
                acc = psum.tile([P, M], F32, name="acc_t", tag="sum")
                product(acc[:], lambda a: table_operand(a, c * P, P), lambda a: weight_operand(a, 0, M))
                scaled[c] = ring.tile([P, M], F32, name="scaled")
                nc.scalar.activation(out=scaled[c][:], in_=acc[:], func=ACT.Copy, scale=ts_col[:, c : c + 1])
        for j0, width in turned:
            for pair in range(N_TILES // 2):
                result = ring.tile([P, 2, width], F32, name="result_t")
                bank = psum.tile([P, 2, width], F32, name="bank_y", tag="sum")
                for h in range(2):
                    n0 = (2 * pair + h) * P
                    for i in range(width // P):
                        nc.tensor.transpose(bank[:, h, i * P : (i + 1) * P], scaled[j0 // P + i][:, n0 : n0 + P], ident[:])
                for h in range(2):
                    t = 2 * pair + h
                    nc.scalar.activation(out=result[:, h, :], in_=bank[:, h, :], func=ACT.Gelu_apprx_tanh, bias=bias[:, t : t + 1])
                store(result, 2 * pair, 2, j0, width)

        for r, (j0, width) in enumerate(direct):
            for t in range(N_TILES):
                acc = psum.tile([P, width], F32, name="acc_d", tag=("turn", "sum")[r % 2])
                product(acc[:], lambda a: weight_operand(a, t * P, P), lambda a: table_operand(a, j0, width))
                y = ring.tile([P, width], F32, name="y", tag="scaled")
                nc.vector.tensor_tensor(out=y[:], in0=acc[:], in1=ts_rows[:, j0 - direct0 : j0 - direct0 + width], op=MULT)
                tiles = 1 if r == len(direct) - 1 else 2
                if t % tiles == 0:
                    result = keep.tile([P, tiles, width], F32, name="result_d%d_%d" % (r, t))
                nc.scalar.activation(out=result[:, t % tiles, :], in_=y[:], func=ACT.Gelu_apprx_tanh, bias=bias[:, t : t + 1])
                if t % tiles == tiles - 1:
                    store(result, t - tiles + 1, tiles, j0, width)
